import numpy as np
import ml_dtypes


def mxq(x, axis, fmt="e4m3"):
    dtype, down = {"e4m3": (ml_dtypes.float8_e4m3fn, 7), "e5m2": (ml_dtypes.float8_e5m2, 14)}[fmt]
    v = np.moveaxis(np.asarray(x, np.float32).astype(ml_dtypes.bfloat16).astype(np.float64), axis, -1)
    blocks = v.reshape(v.shape[:-1] + (-1, 32))
    amax = np.abs(blocks).max(-1, keepdims=True)
    byte = np.maximum(np.where(amax > 0, np.frexp(amax)[1] - 1 + 127, 0) - down, 1)
    scale = np.exp2(byte - 127.0)
    codes = (blocks / scale).astype(np.float32).astype(dtype).astype(np.float64)
    return np.moveaxis((codes * scale).reshape(v.shape), -1, axis)


WIDE = False


def mx_kscale(k):
    if not WIDE:
        return np.ones(k)
    levels = np.array([10, -10, 5, -5, 0])
    if k % 512:
        return np.exp2(np.random.permutation(np.resize(levels, k // 32))).repeat(32)
    a = np.empty((k // 512, 16))
    for p in range(k // 512):
        a[p, :8] = np.random.permutation(np.resize(levels, 8))
        for g in range(8):
            far = levels[np.abs(levels - a[p, g]) >= 10]
            a[p, g + 8] = far[np.random.randint(len(far))]
    return np.exp2(a.ravel()).repeat(32)


BF16 = ml_dtypes.bfloat16


def bf(x):
    return np.asarray(x, np.float32).astype(BF16)


def f64(x):
    return np.asarray(x).astype(np.float64)


E2M1 = np.array([0.0, 0.5, 1.0, 1.5, 2.0, 3.0, 4.0, 6.0, -0.0, -0.5, -1.0, -1.5, -2.0, -3.0, -4.0, -6.0])


def pack_weight(w, fmt):
    k, n = w.shape
    w = f64(bf(w)).reshape(k // 32, 32, n)
    amax = np.abs(w).max(1)
    if fmt == "e4m3":
        byte = np.frexp(amax)[1] - 1 + 127 - 7
    else:
        mant, ex = np.frexp(amax / 6.0)
        byte = np.where(mant > 0.5, ex, ex - 1) + 127
    byte = np.clip(np.where(amax > 0, byte, 1), 1, 254)
    scaled = (w * np.exp2(127.0 - byte)[:, None, :]).reshape(k, n).astype(np.float32)
    by_word = np.ascontiguousarray(scaled.reshape(k // 512, 128, 4, n).transpose(0, 1, 3, 2))
    if fmt == "e4m3":
        words = by_word.astype(ml_dtypes.float8_e4m3fn).view(np.uint8)
    else:
        c = by_word.astype(ml_dtypes.float4_e2m1fn).view(np.uint8) & 0xF
        words = c[..., 0::2] | (c[..., 1::2] << 4)
    return np.ascontiguousarray(words), np.ascontiguousarray(byte.astype(np.uint8).reshape(k // 512, 16, n))


def unpack_weight(words, scales, fmt):
    g, p, n, _ = words.shape
    if fmt == "e4m3":
        vals = np.ascontiguousarray(words).view(ml_dtypes.float8_e4m3fn).astype(np.float64)
    else:
        nib = np.empty((g, p, n, 4), np.uint8)
        nib[..., 0::2] = words & 0xF
        nib[..., 1::2] = words >> 4
        vals = E2M1[nib]
    vals = vals * np.repeat(np.exp2(scales.astype(np.float64) - 127.0), 8, axis=1)[..., None]
    return vals.transpose(0, 1, 3, 2).reshape(g * 512, n)
def pack4(w):
    words, scales = pack_weight(w, "e2m1")
    return words.reshape(words.shape[0], 128, -1), scales


def unpack4(words, scales):
    return unpack_weight(words.reshape(words.shape[0], 128, -1, 2), scales, "e2m1")


T, D, F, R = 2048, 1024, 1024, 512


def draw0():
    s, t = mx_kscale(F), mx_kscale(T)
    x = bf(np.random.standard_normal((T, D)) / t[:, None])
    g = bf(np.random.standard_normal((T, F)) * s[None, :] * t[:, None])
    p = bf(np.random.standard_normal((D, R)))
    lam = bf(np.random.uniform(0.5, 1.5, R))
    q = np.random.standard_normal((R, F)) / np.sqrt(F) / s[None, :]
    q_words, q_scales = pack4(q.T)
    return {
        "x": x,
        "g": g,
        "p": p,
        "lam": lam,
        "q_words": q_words,
        "q_scales": q_scales,
        "avg_i": bf(np.random.uniform(0.2, 1.2, (D, R))),
        "avg_u": bf(np.random.uniform(0.2, 1.2, (D, R))),
    }


def factor_grad(x, g, lam, qt):
    u = mxq(g, 1, "e4m3") @ qt
    ul = u * lam[None, :]
    return (mxq(x, 0, "e4m3").T @ mxq(ul, 0, "e4m3")) / np.sqrt(T)


def core(x, g, p, lam, q_words, q_scales, avg_i, avg_u):
    grad = factor_grad(f64(x), f64(g), f64(lam), unpack4(q_words, q_scales))
    s = np.abs(f64(p) * grad)
    i_new = 0.7 * f64(avg_i) + 0.3 * s
    u_new = 0.7 * f64(avg_u) + 0.3 * np.abs(s - i_new)
    return i_new * u_new


def e4m3fn_bytes(y):
    return np.clip(np.asarray(y, np.float64), -448.0, 448.0).astype(np.float32).astype(ml_dtypes.float8_e4m3fn).view(np.uint8)


def e4m3fn_values(b):
    return np.asarray(b, np.uint8).view(ml_dtypes.float8_e4m3fn).astype(np.float64)


def setup_inputs():
    d = draw0()
    x0 = np.asarray(d['x']).astype(np.float64)
    s = (np.max(np.abs(x0), axis=(1,), keepdims=True) / 448.0).astype(np.float32)
    out = {}
    for k, v in d.items():
        if k == 'x':
            out['x_bytes'] = e4m3fn_bytes(x0 / s.astype(np.float64))
            out['x_scale'] = s
        else:
            out[k] = v
    return out


def reference(x_bytes, x_scale, g, p, lam, q_words, q_scales, avg_i, avg_u):
    return core(e4m3fn_values(x_bytes) * x_scale.astype(np.float64), g, p, lam, q_words, q_scales, avg_i, avg_u)

@@ -1,0 +1,354 @@
+from contextlib import ExitStack
+
+import concourse.mybir as mybir
+from concourse.masks import make_identity
+
+T, D, F, R = 2048, 1024, 1024, 512
+FLOPS = 2 * T * F * R + 2 * T * D * R
+BYTES = T * D + 4 * T + 2 * T * F + 3 * 2 * D * R + 2 * R + F * R // 2 + F * R // 32 + 4 * D * R
+
+F32 = mybir.dt.float32
+BF16 = mybir.dt.bfloat16
+I32 = mybir.dt.int32
+U32 = mybir.dt.uint32
+U8 = mybir.dt.uint8
+FP8 = mybir.dt.float8_e4m3fn
+FP8X4 = mybir.dt.float8_e4m3fn_x4
+FP4X4 = mybir.dt.float4_e2m1fn_x4
+ACT = mybir.ActivationFunctionType
+ALU = mybir.AluOpType
+
+P = 128
+GROUPS = T // 512
+FP = F // 512
+RC = R // 128
+HALF = D // 2
+QUARTER = D // 4
+DT = D // P
+
+
+def tile_adalorasensitivityscore_w4_kernel(tc, x_bytes, x_scale, g, p, lam, q_words, q_scales, avg_i, avg_u, out):
+    nc = tc.nc
+    with ExitStack() as ctx:
+        keep = ctx.enter_context(tc.tile_pool(name="keep", bufs=1))
+        wide = ctx.enter_context(tc.tile_pool(name="wide", bufs=4))
+        work = ctx.enter_context(tc.tile_pool(name="work", bufs=3))
+        ps_t = ctx.enter_context(tc.psum_pool(name="ps_t", bufs=3))
+        ps_u = ctx.enter_context(tc.psum_pool(name="ps_u", bufs=3))
+        ps_g = ctx.enter_context(tc.psum_pool(name="ps_g", bufs=2))
+
+        warm = keep.tile([P, 1], F32, name="warm")
+        lam_row = keep.tile([P, R], BF16, name="lam_row")
+        ones = keep.tile([P, P], BF16, name="ones")
+        ident = keep.tile([P, P], F32, name="ident")
+        ident_b = keep.tile([P, P], BF16, name="ident_b")
+        lam_all = keep.tile([P, R], F32, name="lam_all")
+        x_s = keep.tile([P, GROUPS, 4], F32, name="x_s")
+        q_w = keep.tile([P, FP, 2 * R], U8, align_bytes=64, name="q_w")
+        q_s = keep.tile([P, FP * R], U8, align_bytes=64, name="q_s")
+
+        nc.vector.memset(warm[:], 0.0)
+        nc.vector.memset(q_s[:].bitcast(I32), 0)
+        nc.gpsimd.memset(lam_row[:], 0.0)
+        nc.gpsimd.memset(ones[:], 1.0)
+        make_identity(nc, ident[:])
+        nc.gpsimd.tensor_copy(out=ident_b[:], in_=ident[:])
+        nc.scalar.activation(out=warm[:], in_=warm[:], func=ACT.Abs)
+        nc.scalar.dma_start(out=lam_row[0:1, :], in_=lam.rearrange("(o r) -> o r", o=1))
+
+        x_view = x_bytes.rearrange("(g p t) n -> g p t n", p=P, t=4)
+        g_view = g.rearrange("(g p t) f -> g p t f", p=P, t=4)
+        x_b = [keep.tile([P, 4, D], U8, name=f"x_b{k}") for k in range(GROUPS)]
+        g_sb = [[keep.tile([P, F], BF16, name=f"g_sb{k}_{t}") for t in range(4)] for k in range(GROUPS)]
+        nc.sync.dma_start(out=x_s[:], in_=x_scale.rearrange("(g p t) o -> p g (t o)", p=P, t=4))
+        for k in range(GROUPS):
+            if k == 0:
+                for t in (0, 2):
+                    nc.sync.dma_start(out=x_b[k][:, t : t + 2, :], in_=x_view[k][:, t : t + 2, :])
+            else:
+                nc.sync.dma_start(out=x_b[k][:], in_=x_view[k])
+            for t in range(4):
+                nc.sync.dma_start(out=g_sb[k][t][:], in_=g_view[k][:, t, :])
+            if k == 0:
+                nc.sync.dma_start(out=q_w[:], in_=q_words.rearrange("g p n -> p g n"))
+                for b in range(4):
+                    nc.sync.dma_start(
+                        out=q_s[32 * b : 32 * b + 4, :].bitcast(I32).rearrange("p (g n) -> p g n", g=FP),
+                        in_=q_scales.bitcast(I32).rearrange("g (b r) n -> b r g n", r=4)[b],
+                    )
+        epi = {}
+        for h in range(2):
+            for name, src in (("p", p), ("a", avg_i), ("u", avg_u)):
+                epi[name, h] = keep.tile([P, DT // 2, R], BF16, name=f"{name}_sb{h}")
+                nc.sync.dma_start(
+                    out=epi[name, h][:],
+                    in_=src.rearrange("(h j p) r -> h p j r", p=P, h=2)[h],
+                )
+
+        def rows_of(name, j):
+            return epi[name, j // 4][:, j % 4, :]
+
+        banks = {}
+        g_x = {}
+        g_c = {}
+        g_s = {}
+
+        def turn(k, t):
+            bank = ps_t.tile([P, FP, 2, P], F32, name="bank_t")
+            words = g_sb[k][t][:].bitcast(F32)
+            for f in range(FP):
+                for u in range(2):
+                    nc.tensor.transpose(bank[:, f, u, :], words[:, 256 * f + u : 256 * (f + 1) : 2], ident[:])
+            banks["t", k, t] = bank
+
+        def unload(k, t):
+            if t % 2 == 0:
+                g_x[k, t // 2] = work.tile([P, 2, FP, P, 4], BF16, align_bytes=64, name="g_x")
+            dst = g_x[k, t // 2][:, t % 2].rearrange("p f r t -> p f (r t)").bitcast(F32)
+            nc.scalar.copy(
+                out=dst.rearrange("p f (r u) -> p f r u", u=2),
+                in_=banks["t", k, t][:].rearrange("p f u r -> p f r u"),
+            )
+
+        def quant_g(k, h):
+            codes = work.tile([P, 2, FP, P], U32, align_bytes=64, name=f"g_c{h}")
+            scales = work.tile([P, 2, FP, P], U8, align_bytes=64, name=f"g_s{h}")
+            nc.vector.quantize_mx(
+                out=codes[:].rearrange("p a f r -> p (a f r)").bitcast(FP8X4),
+                scales=scales[:].rearrange("p a f r -> p (a f r)"),
+                in_=g_x[k, h][:].rearrange("p a f r t -> p (a f r t)"),
+            )
+            for a in range(2):
+                g_c[k, 2 * h + a] = codes[:, a]
+                g_s[k, 2 * h + a] = scales[:, a]
+
+        ul_x = {}
+        ul_c = [keep.tile([P, R], U32, align_bytes=64, name=f"ul_c{k}") for k in range(GROUPS)]
+        ul_s = [keep.tile([P, R], U8, align_bytes=64, name=f"ul_s{k}") for k in range(GROUPS)]
+
+        def mul_u(k, c):
+            bank = ps_u.tile([P, 4, P], F32, name="bank_u")
+            for t in range(4):
+                for f in range(FP):
+                    nc.tensor.matmul_mx(
+                        out=bank[:, t, :],
+                        lhsT=g_c[k, t][:, f, :].bitcast(FP8X4),
+                        lhsT_scale=g_s[k, t][:, f, :],
+                        rhs=q_w[:, f, 256 * c : 256 * (c + 1)].bitcast(FP4X4),
+                        rhs_scale=q_s[:, R * f + P * c : R * f + P * (c + 1)],
+                        start=(f == 0),
+                        stop=(f == FP - 1),
+                    )
+            banks["u", k, c] = bank
+
+        def scale_u(k, c):
+            if c == 0:
+                ul_x[k] = work.tile([P, R, 4], BF16, align_bytes=64, name="ul_x")
+            cols = slice(P * c, P * (c + 1))
+            nc.vector.tensor_tensor(
+                out=ul_x[k][:, cols, :],
+                in0=banks["u", k, c][:].rearrange("p t r -> p r t"),
+                in1=lam_all[:, cols].unsqueeze(2).to_broadcast([P, P, 4]),
+                op=ALU.mult,
+            )
+
+        def quant_u(k):
+            nc.vector.quantize_mx(
+                out=ul_c[k][:].bitcast(FP8X4),
+                scales=ul_s[k][:],
+                in_=ul_x[k][:].rearrange("p r t -> p (r t)"),
+            )
+
+        x_w = {}
+        x_x = {}
+        x_c = {}
+        x_q = {}
+
+        def widen(k, t, h, on_vector=False):
+            if t == 0:
+                x_w[k, h] = wide.tile([P, 4, HALF], BF16, align_bytes=64, name=f"x_w{h}")
+            src = x_b[k][:, t, HALF * h : HALF * (h + 1)].bitcast(FP8)
+            dst = x_w[k, h][:, t, :]
+            col = x_s[:, k, t : t + 1]
+            if on_vector:
+                nc.vector.tensor_scalar(out=dst, in0=src, scalar1=col, scalar2=None, op0=ALU.mult)
+            else:
+                nc.scalar.activation(out=dst, in_=src, func=ACT.Copy, scale=col)
+
+        def weave(k, q, on_vector):
+            x_x[k, q] = wide.tile([P, QUARTER, 4], BF16, align_bytes=64, name="x_x")
+            o = QUARTER * (q % 2)
+            src = x_w[k, q // 2][:, :, o : o + QUARTER].rearrange("p t n -> p n t")
+            if on_vector:
+                nc.vector.tensor_copy(out=x_x[k, q][:], in_=src)
+            else:
+                nc.scalar.copy(out=x_x[k, q][:], in_=src)
+
+        def quant_x(k, q):
+            x_c[k, q] = keep.tile([P, QUARTER], U32, align_bytes=64, name=f"x_c{k}_{q}")
+            x_q[k, q] = keep.tile([P, QUARTER], U8, align_bytes=64, name=f"x_q{k}_{q}")
+            nc.vector.quantize_mx(
+                out=x_c[k, q][:].bitcast(FP8X4),
+                scales=x_q[k, q][:],
+                in_=x_x[k, q][:].rearrange("p n t -> p (n t)"),
+            )
+
+        def mul_grad(j, groups):
+            if groups[0] == 0:
+                banks["g", j] = ps_g.tile([P, R], F32, name="bank_g")
+            cols = slice(P * (j % 2), P * (j % 2 + 1))
+            for k in groups:
+                nc.tensor.matmul_mx(
+                    out=banks["g", j][:],
+                    lhsT=x_c[k, j // 2][:, cols].bitcast(FP8X4),
+                    lhsT_scale=x_q[k, j // 2][:, cols],
+                    rhs=ul_c[k][:].bitcast(FP8X4),
+                    rhs_scale=ul_s[k][:],
+                    start=(k == 0),
+                    stop=(k == GROUPS - 1),
+                )
+
+        val = {}
+
+        def times_p(j):
+            y = work.tile([P, R], F32, name="y")
+            nc.vector.tensor_tensor(out=y[:], in0=banks["g", j][:], in1=rows_of("p", j), op=ALU.mult)
+            val["y", j] = y
+
+        def abs_s(j):
+            s = work.tile([P, R], F32, name="s")
+            nc.scalar.activation(out=s[:], in_=val["y", j][:], func=ACT.Abs, scale=3.0 / 7.0 * float(T) ** -0.5)
+            val["s", j] = s
+
+        def diff(j):
+            d = work.tile([P, R], F32, name="d")
+            nc.vector.scalar_tensor_tensor(out=d[:], in0=val["s", j][:], scalar=7.0 / 3.0, in1=banks["a", j][:], op0=ALU.mult, op1=ALU.subtract)
+            val["d", j] = d
+
+        def new_i(j):
+            i = work.tile([P, R], F32, name="i")
+            nc.gpsimd.tensor_tensor(out=i[:], in0=val["s", j][:], in1=rows_of("a", j), op=ALU.add)
+            val["i", j] = i
+
+        def abs_e(j):
+            e = work.tile([P, R], F32, name="e")
+            nc.scalar.activation(out=e[:], in_=val["d", j][:], func=ACT.Abs, scale=0.3)
+            val["e", j] = e
+
+        def new_u(j):
+            w = ps_u.tile([P, R], F32, name="bank_u")
+            nc.tensor.matmul(w[:], ident_b[:], rows_of("u", j), start=True, stop=False)
+            nc.tensor.matmul(w[:], ident[:], val["e", j][:], start=False, stop=True)
+            val["w", j] = w
+
+        def place_a(j):
+            bank = ps_t.tile([P, R], F32, name="bank_t")
+            nc.tensor.matmul(bank[:], ident_b[:], rows_of("a", j), start=True, stop=True)
+            banks["a", j] = bank
+
+        def finish(j):
+            o = work.tile([P, R], F32, name="o")
+            nc.vector.scalar_tensor_tensor(out=o[:], in0=val["w", j][:], scalar=0.49, in1=val["i", j][:], op0=ALU.mult, op1=ALU.mult)
+            nc.sync.dma_start(out=out[P * j : P * (j + 1), :], in_=o[:])
+
+        for t in range(4):
+            widen(0, t, 0, on_vector=True)
+        for t in range(3):
+            turn(0, t)
+        lam_bank = ps_u.tile([P, 4, P], F32, name="bank_u")
+        nc.tensor.matmul(lam_bank[:].rearrange("p t r -> p (t r)"), ones[:], lam_row[:], start=True, stop=True)
+        for t in range(2):
+            unload(0, t)
+        turn(0, 3)
+        weave(0, 0, True)
+        unload(0, 2)
+        nc.scalar.copy(out=lam_all[:], in_=lam_bank[:].rearrange("p t r -> p (t r)"))
+        unload(0, 3)
+        weave(0, 1, True)
+        quant_x(0, 0)
+        quant_g(0, 0)
+        quant_x(0, 1)
+        quant_g(0, 1)
+
+        done = {"n": 0}
+
+        def widen_later(n):
+            for i in range(done["n"], done["n"] + n):
+                widen(i // 4, i % 4, 1)
+            done["n"] += n
+
+        for k in range(GROUPS):
+            n = k + 1
+            more = n < GROUPS
+            mul_u(k, 0)
+            mul_u(k, 1)
+            if more:
+                turn(n, 0)
+                turn(n, 1)
+                widen(n, 0, 0)
+                unload(n, 0)
+                widen(n, 1, 0)
+                unload(n, 1)
+            else:
+                widen_later(4)
+            scale_u(k, 0)
+            scale_u(k, 1)
+            if more:
+                quant_g(n, 0)
+            mul_u(k, 2)
+            mul_u(k, 3)
+            if more:
+                turn(n, 2)
+                turn(n, 3)
+                widen(n, 2, 0)
+                unload(n, 2)
+                widen(n, 3, 0)
+                unload(n, 3)
+                widen_later(3)
+            else:
+                widen_later(3)
+            scale_u(k, 2)
+            scale_u(k, 3)
+            if k > 0:
+                weave(k, 0, True)
+            quant_u(k)
+            if more:
+                quant_g(n, 1)
+            if k > 0:
+                weave(k, 1, True)
+                quant_x(k, 0)
+                quant_x(k, 1)
+
+        for j in range(2):
+            mul_grad(j, range(GROUPS))
+        weave(2, 2, False)
+        weave(3, 2, False)
+        fills = {
+            0: [("w", 0, 2), ("w", 1, 2)],
+            1: [("q", 0, 2), ("q", 1, 2)],
+            2: [("q", 2, 2), ("q", 3, 2)],
+            3: [("q", 0, 3), ("q", 1, 3)],
+            4: [("q", 2, 3), ("q", 3, 3)],
+        }
+        for j in range(DT + 2):
+            if j < DT:
+                place_a(j)
+                times_p(j)
+                abs_s(j)
+            for kind, k, q in fills.get(j, []):
+                if kind == "w":
+                    weave(k, q, True)
+                else:
+                    quant_x(k, q)
+            if j >= 2:
+                new_u(j - 2)
+            if 1 <= j <= DT:
+                diff(j - 1)
+                abs_e(j - 1)
+                new_i(j - 1)
+            if j < GROUPS:
+                weave(j, 3, False)
+            if j >= 2:
+                finish(j - 2)
+            if j + 2 < DT:
+                mul_grad(j + 2, range(GROUPS))

@@ -25,6 +25,8 @@ RC = R // 128
 HALF = D // 2
 QUARTER = D // 4
 DT = D // P
+TENSOR_W = (1, 3, 5)
+GPSIMD_W = ()
 
 
 def tile_adalorasensitivityscore_w4_kernel(tc, x_bytes, x_scale, g, p, lam, q_words, q_scales, avg_i, avg_u, out):
@@ -33,9 +35,9 @@ def tile_adalorasensitivityscore_w4_kernel(tc, x_bytes, x_scale, g, p, lam, q_wo
         keep = ctx.enter_context(tc.tile_pool(name="keep", bufs=1))
         wide = ctx.enter_context(tc.tile_pool(name="wide", bufs=4))
         work = ctx.enter_context(tc.tile_pool(name="work", bufs=3))
-        ps_t = ctx.enter_context(tc.psum_pool(name="ps_t", bufs=3))
-        ps_u = ctx.enter_context(tc.psum_pool(name="ps_u", bufs=3))
-        ps_g = ctx.enter_context(tc.psum_pool(name="ps_g", bufs=2))
+        ps_t = ctx.enter_context(tc.psum_pool(name="ps_t", bufs=4))
+        ps_u = ctx.enter_context(tc.psum_pool(name="ps_u", bufs=4))
+        ctx.enter_context(tc.manual_schedule())
 
         warm = keep.tile([P, 1], F32, name="warm")
         lam_row = keep.tile([P, R], BF16, name="lam_row")
@@ -53,22 +55,22 @@ def tile_adalorasensitivityscore_w4_kernel(tc, x_bytes, x_scale, g, p, lam, q_wo
         nc.gpsimd.memset(ones[:], 1.0)
         make_identity(nc, ident[:])
         nc.gpsimd.tensor_copy(out=ident_b[:], in_=ident[:])
-        nc.scalar.activation(out=warm[:], in_=warm[:], func=ACT.Abs)
+        nc.scalar.dma_start(out=x_s[:], in_=x_scale.rearrange("(g p t) o -> p g (t o)", p=P, t=4))
         nc.scalar.dma_start(out=lam_row[0:1, :], in_=lam.rearrange("(o r) -> o r", o=1))
+        nc.scalar.activation(out=warm[:], in_=warm[:], func=ACT.Abs)
 
         x_view = x_bytes.rearrange("(g p t) n -> g p t n", p=P, t=4)
         g_view = g.rearrange("(g p t) f -> g p t f", p=P, t=4)
         x_b = [keep.tile([P, 4, D], U8, name=f"x_b{k}") for k in range(GROUPS)]
         g_sb = [[keep.tile([P, F], BF16, name=f"g_sb{k}_{t}") for t in range(4)] for k in range(GROUPS)]
-        nc.sync.dma_start(out=x_s[:], in_=x_scale.rearrange("(g p t) o -> p g (t o)", p=P, t=4))
         for k in range(GROUPS):
             if k == 0:
-                for t in (0, 2):
-                    nc.sync.dma_start(out=x_b[k][:, t : t + 2, :], in_=x_view[k][:, t : t + 2, :])
-            else:
-                nc.sync.dma_start(out=x_b[k][:], in_=x_view[k])
+                for t0, t1 in ((0, 1), (1, 2), (2, 4)):
+                    nc.sync.dma_start(out=x_b[k][:, t0:t1, :], in_=x_view[k][:, t0:t1, :])
             for t in range(4):
                 nc.sync.dma_start(out=g_sb[k][t][:], in_=g_view[k][:, t, :])
+            if k > 0:
+                nc.sync.dma_start(out=x_b[k][:], in_=x_view[k])
             if k == 0:
                 nc.sync.dma_start(out=q_w[:], in_=q_words.rearrange("g p n -> p g n"))
                 for b in range(4):
@@ -166,7 +168,7 @@ def tile_adalorasensitivityscore_w4_kernel(tc, x_bytes, x_scale, g, p, lam, q_wo
 
         def widen(k, t, h, on_vector=False):
             if t == 0:
-                x_w[k, h] = wide.tile([P, 4, HALF], BF16, align_bytes=64, name=f"x_w{h}")
+                x_w[k, h] = (work, wide)[h].tile([P, 4, HALF], BF16, align_bytes=64, name=f"x_w{h}")
             src = x_b[k][:, t, HALF * h : HALF * (h + 1)].bitcast(FP8)
             dst = x_w[k, h][:, t, :]
             col = x_s[:, k, t : t + 1]
@@ -175,33 +177,39 @@ def tile_adalorasensitivityscore_w4_kernel(tc, x_bytes, x_scale, g, p, lam, q_wo
             else:
                 nc.scalar.activation(out=dst, in_=src, func=ACT.Copy, scale=col)
 
-        def weave(k, q, on_vector):
-            x_x[k, q] = wide.tile([P, QUARTER, 4], BF16, align_bytes=64, name="x_x")
-            o = QUARTER * (q % 2)
-            src = x_w[k, q // 2][:, :, o : o + QUARTER].rearrange("p t n -> p n t")
+        def weave(k, j0, j1, on_vector):
+            n = P * (j1 - j0)
+            x_x[k, j0] = work.tile([P, n, 4], BF16, align_bytes=64, name=f"x_x{j1 - j0}")
+            o = P * (j0 % 4)
+            src = x_w[k, j0 // 4][:, :, o : o + n].rearrange("p t (n i) -> p n t i", i=4)
+            dst = x_x[k, j0][:].rearrange("p (n i) t -> p n t i", i=4)
             if on_vector:
-                nc.vector.tensor_copy(out=x_x[k, q][:], in_=src)
+                nc.vector.tensor_copy(out=dst, in_=src)
             else:
-                nc.scalar.copy(out=x_x[k, q][:], in_=src)
+                nc.scalar.copy(out=dst, in_=src)
 
-        def quant_x(k, q):
-            x_c[k, q] = keep.tile([P, QUARTER], U32, align_bytes=64, name=f"x_c{k}_{q}")
-            x_q[k, q] = keep.tile([P, QUARTER], U8, align_bytes=64, name=f"x_q{k}_{q}")
+        def quant_x(k, j0, j1):
+            n = P * (j1 - j0)
+            codes = keep.tile([P, n], U32, align_bytes=64, name=f"x_c{k}_{j0}")
+            scales = keep.tile([P, n], U8, align_bytes=64, name=f"x_q{k}_{j0}")
             nc.vector.quantize_mx(
-                out=x_c[k, q][:].bitcast(FP8X4),
-                scales=x_q[k, q][:],
-                in_=x_x[k, q][:].rearrange("p n t -> p (n t)"),
+                out=codes[:].bitcast(FP8X4),
+                scales=scales[:],
+                in_=x_x[k, j0][:].rearrange("p n t -> p (n t)"),
             )
+            for j in range(j0, j1):
+                cols = slice(P * (j - j0), P * (j - j0 + 1))
+                x_c[k, j] = codes[:, cols]
+                x_q[k, j] = scales[:, cols]
 
         def mul_grad(j, groups):
             if groups[0] == 0:
-                banks["g", j] = ps_g.tile([P, R], F32, name="bank_g")
-            cols = slice(P * (j % 2), P * (j % 2 + 1))
+                banks["g", j] = ps_u.tile([P, R], F32, name="bank_u")
             for k in groups:
                 nc.tensor.matmul_mx(
                     out=banks["g", j][:],
-                    lhsT=x_c[k, j // 2][:, cols].bitcast(FP8X4),
-                    lhsT_scale=x_q[k, j // 2][:, cols],
+                    lhsT=x_c[k, j].bitcast(FP8X4),
+                    lhsT_scale=x_q[k, j],
                     rhs=ul_c[k][:].bitcast(FP8X4),
                     rhs_scale=ul_s[k][:],
                     start=(k == 0),
@@ -235,10 +243,22 @@ def tile_adalorasensitivityscore_w4_kernel(tc, x_bytes, x_scale, g, p, lam, q_wo
             nc.scalar.activation(out=e[:], in_=val["d", j][:], func=ACT.Abs, scale=0.3)
             val["e", j] = e
 
+        def place_u(j):
+            bank = ps_u.tile([P, R], F32, name="bank_u")
+            nc.tensor.matmul(bank[:], ident_b[:], rows_of("u", j), start=True, stop=True)
+            banks["w", j] = bank
+
         def new_u(j):
-            w = ps_u.tile([P, R], F32, name="bank_u")
-            nc.tensor.matmul(w[:], ident_b[:], rows_of("u", j), start=True, stop=False)
-            nc.tensor.matmul(w[:], ident[:], val["e", j][:], start=False, stop=True)
+            if j in TENSOR_W:
+                w = ps_t.tile([P, R], F32, name="bank_t")
+                nc.tensor.matmul(w[:], ident_b[:], rows_of("u", j), start=True, stop=False)
+                nc.tensor.matmul(w[:], ident[:], val["e", j][:], start=False, stop=True)
+            else:
+                w = work.tile([P, R], F32, name="w")
+                if j in GPSIMD_W:
+                    nc.gpsimd.tensor_tensor(out=w[:], in0=val["e", j][:], in1=rows_of("u", j), op=ALU.add)
+                else:
+                    nc.vector.tensor_tensor(out=w[:], in0=banks["w", j][:], in1=val["e", j][:], op=ALU.add)
             val["w", j] = w
 
         def place_a(j):
@@ -251,104 +271,88 @@ def tile_adalorasensitivityscore_w4_kernel(tc, x_bytes, x_scale, g, p, lam, q_wo
             nc.vector.scalar_tensor_tensor(out=o[:], in0=val["w", j][:], scalar=0.49, in1=val["i", j][:], op0=ALU.mult, op1=ALU.mult)
             nc.sync.dma_start(out=out[P * j : P * (j + 1), :], in_=o[:])
 
-        for t in range(4):
-            widen(0, t, 0, on_vector=True)
-        for t in range(3):
-            turn(0, t)
         lam_bank = ps_u.tile([P, 4, P], F32, name="bank_u")
         nc.tensor.matmul(lam_bank[:].rearrange("p t r -> p (t r)"), ones[:], lam_row[:], start=True, stop=True)
-        for t in range(2):
+        for t in range(4):
+            widen(0, t, 0, on_vector=True)
+        widen(0, 0, 1)
+        widen(0, 1, 1)
+        widen(0, 2, 1)
+        for t in range(4):
+            turn(0, t)
             unload(0, t)
-        turn(0, 3)
-        weave(0, 0, True)
-        unload(0, 2)
         nc.scalar.copy(out=lam_all[:], in_=lam_bank[:].rearrange("p t r -> p (t r)"))
-        unload(0, 3)
-        weave(0, 1, True)
-        quant_x(0, 0)
+        weave(0, 0, 4, True)
+        quant_x(0, 0, 4)
+        widen(0, 3, 1, on_vector=True)
         quant_g(0, 0)
-        quant_x(0, 1)
+        weave(0, 4, 6, True)
         quant_g(0, 1)
-
-        done = {"n": 0}
-
-        def widen_later(n):
-            for i in range(done["n"], done["n"] + n):
-                widen(i // 4, i % 4, 1)
-            done["n"] += n
+        quant_x(0, 4, 6)
 
         for k in range(GROUPS):
             n = k + 1
             more = n < GROUPS
+            if more:
+                for t in range(4):
+                    turn(n, t)
+                for t in range(2):
+                    unload(n, t)
             mul_u(k, 0)
             mul_u(k, 1)
-            if more:
-                turn(n, 0)
-                turn(n, 1)
-                widen(n, 0, 0)
-                unload(n, 0)
-                widen(n, 1, 0)
-                unload(n, 1)
+            if k == 0:
+                weave(0, 6, 8, True)
+                quant_x(0, 6, 8)
+            elif k < 3:
+                weave(k, 0, 4, True)
+                quant_x(k, 0, 4)
             else:
-                widen_later(4)
-            scale_u(k, 0)
-            scale_u(k, 1)
-            if more:
-                quant_g(n, 0)
+                weave(k, 0, 2, True)
+                quant_x(k, 0, 2)
             mul_u(k, 2)
             mul_u(k, 3)
             if more:
-                turn(n, 2)
-                turn(n, 3)
-                widen(n, 2, 0)
+                quant_g(n, 0)
                 unload(n, 2)
-                widen(n, 3, 0)
                 unload(n, 3)
-                widen_later(3)
-            else:
-                widen_later(3)
-            scale_u(k, 2)
-            scale_u(k, 3)
-            if k > 0:
-                weave(k, 0, True)
-            quant_u(k)
+            for c in range(4):
+                scale_u(k, c)
             if more:
+                for t in range(4):
+                    widen(n, t, 0)
                 quant_g(n, 1)
-            if k > 0:
-                weave(k, 1, True)
-                quant_x(k, 0)
-                quant_x(k, 1)
+                for t in range(2):
+                    widen(n, t, 1)
+            quant_u(k)
 
+        weave(3, 2, 4, True)
+        quant_x(3, 2, 4)
         for j in range(2):
             mul_grad(j, range(GROUPS))
-        weave(2, 2, False)
-        weave(3, 2, False)
-        fills = {
-            0: [("w", 0, 2), ("w", 1, 2)],
-            1: [("q", 0, 2), ("q", 1, 2)],
-            2: [("q", 2, 2), ("q", 3, 2)],
-            3: [("q", 0, 3), ("q", 1, 3)],
-            4: [("q", 2, 3), ("q", 3, 3)],
-        }
-        for j in range(DT + 2):
+        for k in range(1, GROUPS):
+            for t in range(2, 4):
+                widen(k, t, 1)
+            weave(k, 4, 6, k in ())
+        weaves = {1: [(1, 6, 8)], 2: [(2, 6, 8)], 3: [(3, 6, 8)]}
+        quants = {0: [(1, 4, 6)], 1: [(2, 4, 6), (3, 4, 6)], 2: [(1, 6, 8)], 3: [(2, 6, 8)], 4: [(3, 6, 8)]}
+        for j in range(DT + 3):
             if j < DT:
-                place_a(j)
                 times_p(j)
                 abs_s(j)
-            for kind, k, q in fills.get(j, []):
-                if kind == "w":
-                    weave(k, q, True)
-                else:
-                    quant_x(k, q)
-            if j >= 2:
+                place_a(j)
+            if 2 <= j < DT + 2:
                 new_u(j - 2)
+            if j < DT and j not in TENSOR_W and j not in GPSIMD_W:
+                place_u(j)
             if 1 <= j <= DT:
+                new_i(j - 1)
                 diff(j - 1)
                 abs_e(j - 1)
-                new_i(j - 1)
-            if j < GROUPS:
-                weave(j, 3, False)
-            if j >= 2:
-                finish(j - 2)
+            if j >= 3:
+                finish(j - 3)
+            for unit in weaves.get(j, []):
+                weave(*unit, False)
+            for unit in quants.get(j, []):
+                quant_x(*unit)
             if j + 2 < DT:
                 mul_grad(j + 2, range(GROUPS))

@@ -19,21 +19,22 @@ ACT = mybir.ActivationFunctionType
 ALU = mybir.AluOpType
 
 P = 128
+PACK = 4
 GROUPS = T // 512
 FP = F // 512
-RC = R // 128
-HALF = D // 2
-QUARTER = D // 4
 DT = D // P
-TENSOR_W = (1, 3, 5)
-GPSIMD_W = ()
+HALF = D // 2
+TENSOR_W = (0, 2, 3, 5, 6)
+WIDE = (0, 2, 2, 2)
+SQRT_T_INV = float(T) ** -0.5
 
 
 def tile_adalorasensitivityscore_w4_kernel(tc, x_bytes, x_scale, g, p, lam, q_words, q_scales, avg_i, avg_u, out):
     nc = tc.nc
     with ExitStack() as ctx:
         keep = ctx.enter_context(tc.tile_pool(name="keep", bufs=1))
-        wide = ctx.enter_context(tc.tile_pool(name="wide", bufs=4))
+        pair = ctx.enter_context(tc.tile_pool(name="pair", bufs=2))
+        quad = ctx.enter_context(tc.tile_pool(name="quad", bufs=4))
         work = ctx.enter_context(tc.tile_pool(name="work", bufs=3))
         ps_t = ctx.enter_context(tc.psum_pool(name="ps_t", bufs=4))
         ps_u = ctx.enter_context(tc.psum_pool(name="ps_u", bufs=4))
@@ -45,7 +46,7 @@ def tile_adalorasensitivityscore_w4_kernel(tc, x_bytes, x_scale, g, p, lam, q_wo
         ident = keep.tile([P, P], F32, name="ident")
         ident_b = keep.tile([P, P], BF16, name="ident_b")
         lam_all = keep.tile([P, R], F32, name="lam_all")
-        x_s = keep.tile([P, GROUPS, 4], F32, name="x_s")
+        x_s = keep.tile([P, GROUPS, PACK], F32, name="x_s")
         q_w = keep.tile([P, FP, 2 * R], U8, align_bytes=64, name="q_w")
         q_s = keep.tile([P, FP * R], U8, align_bytes=64, name="q_s")
 
@@ -55,23 +56,22 @@ def tile_adalorasensitivityscore_w4_kernel(tc, x_bytes, x_scale, g, p, lam, q_wo
         nc.gpsimd.memset(ones[:], 1.0)
         make_identity(nc, ident[:])
         nc.gpsimd.tensor_copy(out=ident_b[:], in_=ident[:])
-        nc.scalar.dma_start(out=x_s[:], in_=x_scale.rearrange("(g p t) o -> p g (t o)", p=P, t=4))
+        nc.scalar.dma_start(out=x_s[:], in_=x_scale.rearrange("(g p t) o -> p g (t o)", p=P, t=PACK))
         nc.scalar.dma_start(out=lam_row[0:1, :], in_=lam.rearrange("(o r) -> o r", o=1))
         nc.scalar.activation(out=warm[:], in_=warm[:], func=ACT.Abs)
 
-        x_view = x_bytes.rearrange("(g p t) n -> g p t n", p=P, t=4)
-        g_view = g.rearrange("(g p t) f -> g p t f", p=P, t=4)
-        x_b = [keep.tile([P, 4, D], U8, name=f"x_b{k}") for k in range(GROUPS)]
-        g_sb = [[keep.tile([P, F], BF16, name=f"g_sb{k}_{t}") for t in range(4)] for k in range(GROUPS)]
+        x_view = x_bytes.rearrange("(g p t) n -> g p t n", p=P, t=PACK)
+        g_view = g.rearrange("(g p t) f -> g p t f", p=P, t=PACK)
+        x_b = [keep.tile([P, PACK, D], U8, name=f"x_b{k}") for k in range(GROUPS)]
+        g_sb = [[keep.tile([P, F], BF16, name=f"g_sb{k}_{t}") for t in range(PACK)] for k in range(GROUPS)]
+        for t0, t1 in ((0, 1), (1, 2), (2, 4)):
+            nc.sync.dma_start(out=x_b[0][:, t0:t1, :], in_=x_view[0][:, t0:t1, :])
         for k in range(GROUPS):
-            if k == 0:
-                for t0, t1 in ((0, 1), (1, 2), (2, 4)):
-                    nc.sync.dma_start(out=x_b[k][:, t0:t1, :], in_=x_view[k][:, t0:t1, :])
-            for t in range(4):
+            for t in range(PACK):
                 nc.sync.dma_start(out=g_sb[k][t][:], in_=g_view[k][:, t, :])
             if k > 0:
                 nc.sync.dma_start(out=x_b[k][:], in_=x_view[k])
-            if k == 0:
+            else:
                 nc.sync.dma_start(out=q_w[:], in_=q_words.rearrange("g p n -> p g n"))
                 for b in range(4):
                     nc.sync.dma_start(
@@ -82,75 +82,70 @@ def tile_adalorasensitivityscore_w4_kernel(tc, x_bytes, x_scale, g, p, lam, q_wo
         for h in range(2):
             for name, src in (("p", p), ("a", avg_i), ("u", avg_u)):
                 epi[name, h] = keep.tile([P, DT // 2, R], BF16, name=f"{name}_sb{h}")
-                nc.sync.dma_start(
-                    out=epi[name, h][:],
-                    in_=src.rearrange("(h j p) r -> h p j r", p=P, h=2)[h],
-                )
+                nc.sync.dma_start(out=epi[name, h][:], in_=src.rearrange("(h j p) r -> h p j r", p=P, h=2)[h])
 
         def rows_of(name, j):
             return epi[name, j // 4][:, j % 4, :]
 
-        banks = {}
+        turned = {}
         g_x = {}
         g_c = {}
         g_s = {}
 
-        def turn(k, t):
+        def turn_g(k, t):
             bank = ps_t.tile([P, FP, 2, P], F32, name="bank_t")
             words = g_sb[k][t][:].bitcast(F32)
             for f in range(FP):
                 for u in range(2):
                     nc.tensor.transpose(bank[:, f, u, :], words[:, 256 * f + u : 256 * (f + 1) : 2], ident[:])
-            banks["t", k, t] = bank
+            turned[k, t] = bank
 
-        def unload(k, t):
-            if t % 2 == 0:
-                g_x[k, t // 2] = work.tile([P, 2, FP, P, 4], BF16, align_bytes=64, name="g_x")
-            dst = g_x[k, t // 2][:, t % 2].rearrange("p f r t -> p f (r t)").bitcast(F32)
+        def unload_g(k, t):
+            if t == 0:
+                g_x[k] = pair.tile([P, PACK, FP, P, PACK], BF16, align_bytes=64, name="g_x")
+            dst = g_x[k][:, t].rearrange("p f r t -> p f (r t)").bitcast(F32)
             nc.scalar.copy(
                 out=dst.rearrange("p f (r u) -> p f r u", u=2),
-                in_=banks["t", k, t][:].rearrange("p f u r -> p f r u"),
+                in_=turned[k, t][:].rearrange("p f u r -> p f r u"),
             )
 
-        def quant_g(k, h):
-            codes = work.tile([P, 2, FP, P], U32, align_bytes=64, name=f"g_c{h}")
-            scales = work.tile([P, 2, FP, P], U8, align_bytes=64, name=f"g_s{h}")
+        def quant_g(k):
+            g_c[k] = pair.tile([P, PACK, FP, P], U32, align_bytes=64, name="g_c")
+            g_s[k] = pair.tile([P, PACK, FP, P], U8, align_bytes=64, name="g_s")
             nc.vector.quantize_mx(
-                out=codes[:].rearrange("p a f r -> p (a f r)").bitcast(FP8X4),
-                scales=scales[:].rearrange("p a f r -> p (a f r)"),
-                in_=g_x[k, h][:].rearrange("p a f r t -> p (a f r t)"),
+                out=g_c[k][:].rearrange("p a f r -> p (a f r)").bitcast(FP8X4),
+                scales=g_s[k][:].rearrange("p a f r -> p (a f r)"),
+                in_=g_x[k][:].rearrange("p a f r t -> p (a f r t)"),
             )
-            for a in range(2):
-                g_c[k, 2 * h + a] = codes[:, a]
-                g_s[k, 2 * h + a] = scales[:, a]
 
+        u_bank = {}
         ul_x = {}
         ul_c = [keep.tile([P, R], U32, align_bytes=64, name=f"ul_c{k}") for k in range(GROUPS)]
         ul_s = [keep.tile([P, R], U8, align_bytes=64, name=f"ul_s{k}") for k in range(GROUPS)]
 
         def mul_u(k, c):
-            bank = ps_u.tile([P, 4, P], F32, name="bank_u")
-            for t in range(4):
+            bank = ps_u.tile([P, PACK, P], F32, name="bank_u")
+            for t in range(PACK):
                 for f in range(FP):
                     nc.tensor.matmul_mx(
                         out=bank[:, t, :],
-                        lhsT=g_c[k, t][:, f, :].bitcast(FP8X4),
-                        lhsT_scale=g_s[k, t][:, f, :],
-                        rhs=q_w[:, f, 256 * c : 256 * (c + 1)].bitcast(FP4X4),
+                        lhsT=g_c[k][:, t, f, :].bitcast(FP8X4),
+                        lhsT_scale=g_s[k][:, t, f, :],
+                        rhs=q_w[:, f, 2 * P * c : 2 * P * (c + 1)].bitcast(FP4X4),
                         rhs_scale=q_s[:, R * f + P * c : R * f + P * (c + 1)],
                         start=(f == 0),
                         stop=(f == FP - 1),
                     )
-            banks["u", k, c] = bank
+            u_bank[k, c] = bank
 
         def scale_u(k, c):
             if c == 0:
-                ul_x[k] = work.tile([P, R, 4], BF16, align_bytes=64, name="ul_x")
+                ul_x[k] = pair.tile([P, R, PACK], BF16, align_bytes=64, name="ul_x")
             cols = slice(P * c, P * (c + 1))
             nc.vector.tensor_tensor(
                 out=ul_x[k][:, cols, :],
-                in0=banks["u", k, c][:].rearrange("p t r -> p r t"),
-                in1=lam_all[:, cols].unsqueeze(2).to_broadcast([P, P, 4]),
+                in0=u_bank[k, c][:].rearrange("p t r -> p r t"),
+                in1=lam_all[:, cols].unsqueeze(2).to_broadcast([P, P, PACK]),
                 op=ALU.mult,
             )
 
@@ -161,16 +156,15 @@ def tile_adalorasensitivityscore_w4_kernel(tc, x_bytes, x_scale, g, p, lam, q_wo
                 in_=ul_x[k][:].rearrange("p r t -> p (r t)"),
             )
 
-        x_w = {}
+        x_w = [keep.tile([P, PACK, D], BF16, align_bytes=64, name=f"x_w{k}") for k in range(GROUPS)]
         x_x = {}
         x_c = {}
         x_q = {}
 
-        def widen(k, t, h, on_vector=False):
-            if t == 0:
-                x_w[k, h] = (work, wide)[h].tile([P, 4, HALF], BF16, align_bytes=64, name=f"x_w{h}")
-            src = x_b[k][:, t, HALF * h : HALF * (h + 1)].bitcast(FP8)
-            dst = x_w[k, h][:, t, :]
+        def widen(k, t, h0, h1, on_vector=False):
+            cols = slice(HALF * h0, HALF * h1)
+            src = x_b[k][:, t, cols].bitcast(FP8)
+            dst = x_w[k][:, t, cols]
             col = x_s[:, k, t : t + 1]
             if on_vector:
                 nc.vector.tensor_scalar(out=dst, in0=src, scalar1=col, scalar2=None, op0=ALU.mult)
@@ -179,9 +173,9 @@ def tile_adalorasensitivityscore_w4_kernel(tc, x_bytes, x_scale, g, p, lam, q_wo
 
         def weave(k, j0, j1, on_vector):
             n = P * (j1 - j0)
-            x_x[k, j0] = work.tile([P, n, 4], BF16, align_bytes=64, name=f"x_x{j1 - j0}")
-            o = P * (j0 % 4)
-            src = x_w[k, j0 // 4][:, :, o : o + n].rearrange("p t (n i) -> p n t i", i=4)
+            if (k, j0) not in x_x:
+                x_x[k, j0] = (quad, pair)[n == HALF].tile([P, n, PACK], BF16, align_bytes=64, name=f"x_x{j1 - j0}")
+            src = x_w[k][:, :, P * j0 : P * j1].rearrange("p t (n i) -> p n t i", i=4)
             dst = x_x[k, j0][:].rearrange("p (n i) t -> p n t i", i=4)
             if on_vector:
                 nc.vector.tensor_copy(out=dst, in_=src)
@@ -202,12 +196,17 @@ def tile_adalorasensitivityscore_w4_kernel(tc, x_bytes, x_scale, g, p, lam, q_wo
                 x_c[k, j] = codes[:, cols]
                 x_q[k, j] = scales[:, cols]
 
+        grad = {}
+        a_bank = {}
+        u_new = {}
+        y, s, d, e, i_new = {}, {}, {}, {}, {}
+
         def mul_grad(j, groups):
             if groups[0] == 0:
-                banks["g", j] = ps_u.tile([P, R], F32, name="bank_u")
+                grad[j] = ps_u.tile([P, R], F32, name="bank_u")
             for k in groups:
                 nc.tensor.matmul_mx(
-                    out=banks["g", j][:],
+                    out=grad[j][:],
                     lhsT=x_c[k, j].bitcast(FP8X4),
                     lhsT_scale=x_q[k, j],
                     rhs=ul_c[k][:].bitcast(FP8X4),
@@ -216,124 +215,108 @@ def tile_adalorasensitivityscore_w4_kernel(tc, x_bytes, x_scale, g, p, lam, q_wo
                     stop=(k == GROUPS - 1),
                 )
 
-        val = {}
-
         def times_p(j):
-            y = work.tile([P, R], F32, name="y")
-            nc.vector.tensor_tensor(out=y[:], in0=banks["g", j][:], in1=rows_of("p", j), op=ALU.mult)
-            val["y", j] = y
+            y[j] = work.tile([P, R], F32, name="y")
+            nc.vector.tensor_tensor(out=y[j][:], in0=grad[j][:], in1=rows_of("p", j), op=ALU.mult)
 
         def abs_s(j):
-            s = work.tile([P, R], F32, name="s")
-            nc.scalar.activation(out=s[:], in_=val["y", j][:], func=ACT.Abs, scale=3.0 / 7.0 * float(T) ** -0.5)
-            val["s", j] = s
+            s[j] = work.tile([P, R], F32, name="s")
+            nc.scalar.activation(out=s[j][:], in_=y[j][:], func=ACT.Abs, scale=3.0 / 7.0 * SQRT_T_INV)
 
-        def diff(j):
-            d = work.tile([P, R], F32, name="d")
-            nc.vector.scalar_tensor_tensor(out=d[:], in0=val["s", j][:], scalar=7.0 / 3.0, in1=banks["a", j][:], op0=ALU.mult, op1=ALU.subtract)
-            val["d", j] = d
+        def place_a(j):
+            a_bank[j] = ps_t.tile([P, R], F32, name="bank_t")
+            nc.tensor.matmul(a_bank[j][:], ident_b[:], rows_of("a", j), start=True, stop=True)
 
-        def new_i(j):
-            i = work.tile([P, R], F32, name="i")
-            nc.gpsimd.tensor_tensor(out=i[:], in0=val["s", j][:], in1=rows_of("a", j), op=ALU.add)
-            val["i", j] = i
+        def add_a(j):
+            i_new[j] = work.tile([P, R], F32, name="i_new")
+            nc.gpsimd.tensor_tensor(out=i_new[j][:], in0=s[j][:], in1=rows_of("a", j), op=ALU.add)
+
+        def minus_a(j):
+            d[j] = work.tile([P, R], F32, name="d")
+            nc.vector.scalar_tensor_tensor(out=d[j][:], in0=s[j][:], scalar=7.0 / 3.0, in1=a_bank[j][:], op0=ALU.mult, op1=ALU.subtract)
 
         def abs_e(j):
-            e = work.tile([P, R], F32, name="e")
-            nc.scalar.activation(out=e[:], in_=val["d", j][:], func=ACT.Abs, scale=0.3)
-            val["e", j] = e
+            e[j] = work.tile([P, R], F32, name="e")
+            nc.scalar.activation(out=e[j][:], in_=d[j][:], func=ACT.Abs, scale=0.3)
 
         def place_u(j):
-            bank = ps_u.tile([P, R], F32, name="bank_u")
-            nc.tensor.matmul(bank[:], ident_b[:], rows_of("u", j), start=True, stop=True)
-            banks["w", j] = bank
+            u_new[j] = ps_u.tile([P, R], F32, name="bank_u")
+            nc.tensor.matmul(u_new[j][:], ident_b[:], rows_of("u", j), start=True, stop=True)
 
-        def new_u(j):
+        def add_u(j):
             if j in TENSOR_W:
                 w = ps_t.tile([P, R], F32, name="bank_t")
                 nc.tensor.matmul(w[:], ident_b[:], rows_of("u", j), start=True, stop=False)
-                nc.tensor.matmul(w[:], ident[:], val["e", j][:], start=False, stop=True)
+                nc.tensor.matmul(w[:], ident[:], e[j][:], start=False, stop=True)
             else:
-                w = work.tile([P, R], F32, name="w")
-                if j in GPSIMD_W:
-                    nc.gpsimd.tensor_tensor(out=w[:], in0=val["e", j][:], in1=rows_of("u", j), op=ALU.add)
-                else:
-                    nc.vector.tensor_tensor(out=w[:], in0=banks["w", j][:], in1=val["e", j][:], op=ALU.add)
-            val["w", j] = w
-
-        def place_a(j):
-            bank = ps_t.tile([P, R], F32, name="bank_t")
-            nc.tensor.matmul(bank[:], ident_b[:], rows_of("a", j), start=True, stop=True)
-            banks["a", j] = bank
+                w = pair.tile([P, R], F32, name="w")
+                nc.vector.tensor_tensor(out=w[:], in0=u_new[j][:], in1=e[j][:], op=ALU.add)
+            u_new[j] = w
 
         def finish(j):
             o = work.tile([P, R], F32, name="o")
-            nc.vector.scalar_tensor_tensor(out=o[:], in0=val["w", j][:], scalar=0.49, in1=val["i", j][:], op0=ALU.mult, op1=ALU.mult)
-            nc.sync.dma_start(out=out[P * j : P * (j + 1), :], in_=o[:])
+            parts = 2 if j == DT - 1 else 1
+            for i in range(parts):
+                cols = slice(R // parts * i, R // parts * (i + 1))
+                nc.vector.scalar_tensor_tensor(
+                    out=o[:, cols], in0=u_new[j][:, cols], scalar=0.49, in1=i_new[j][:, cols], op0=ALU.mult, op1=ALU.mult
+                )
+                nc.sync.dma_start(out=out[P * j : P * (j + 1), cols], in_=o[:, cols])
 
-        lam_bank = ps_u.tile([P, 4, P], F32, name="bank_u")
-        nc.tensor.matmul(lam_bank[:].rearrange("p t r -> p (t r)"), ones[:], lam_row[:], start=True, stop=True)
-        for t in range(4):
-            widen(0, t, 0, on_vector=True)
-        widen(0, 0, 1)
-        widen(0, 1, 1)
-        widen(0, 2, 1)
-        for t in range(4):
-            turn(0, t)
-            unload(0, t)
-        nc.scalar.copy(out=lam_all[:], in_=lam_bank[:].rearrange("p t r -> p (t r)"))
+        lam_bank = ps_u.tile([P, R], F32, name="bank_u")
+        nc.tensor.matmul(lam_bank[:], ones[:], lam_row[:], start=True, stop=True)
+        for t in range(PACK):
+            widen(0, t, 0, 1, on_vector=True)
+        for t in range(3):
+            widen(0, t, 1, 2)
+        for t in range(PACK):
+            turn_g(0, t)
+            unload_g(0, t)
+        nc.scalar.copy(out=lam_all[:], in_=lam_bank[:])
         weave(0, 0, 4, True)
+        widen(0, 3, 1, 2, on_vector=True)
         quant_x(0, 0, 4)
-        widen(0, 3, 1, on_vector=True)
-        quant_g(0, 0)
-        weave(0, 4, 6, True)
-        quant_g(0, 1)
-        quant_x(0, 4, 6)
+        weave(0, 4, 8, True)
+        quant_g(0)
+        quant_x(0, 4, 8)
 
         for k in range(GROUPS):
             n = k + 1
-            more = n < GROUPS
-            if more:
-                for t in range(4):
-                    turn(n, t)
-                for t in range(2):
-                    unload(n, t)
-            mul_u(k, 0)
-            mul_u(k, 1)
-            if k == 0:
-                weave(0, 6, 8, True)
-                quant_x(0, 6, 8)
-            elif k < 3:
-                weave(k, 0, 4, True)
-                quant_x(k, 0, 4)
-            else:
-                weave(k, 0, 2, True)
-                quant_x(k, 0, 2)
-            mul_u(k, 2)
-            mul_u(k, 3)
-            if more:
-                quant_g(n, 0)
-                unload(n, 2)
-                unload(n, 3)
+            if n < GROUPS:
+                for t in range(PACK):
+                    turn_g(n, t)
+                    unload_g(n, t)
+                    if n > 1 and t in (1,):
+                        widen(n, t, 0, 2 if t < WIDE[n] else 1)
+                for t in range(PACK):
+                    if n == 1 or t not in (1,):
+                        widen(n, t, 0, 2 if t < WIDE[n] else 1)
             for c in range(4):
-                scale_u(k, c)
-            if more:
-                for t in range(4):
-                    widen(n, t, 0)
-                quant_g(n, 1)
-                for t in range(2):
-                    widen(n, t, 1)
+                mul_u(k, c)
+            if k > 0:
+                weave(k, 0, 4 if k < 3 else 2, True)
+            scale_u(k, 0)
+            scale_u(k, 1)
+            if k > 0:
+                quant_x(k, 0, 4 if k < 3 else 2)
+            if k == 3:
+                mul_grad(0, range(3))
+                mul_grad(1, range(3))
+            scale_u(k, 2)
+            scale_u(k, 3)
+            if n < GROUPS:
+                quant_g(n)
+            else:
+                weave(3, 2, 4, True)
             quant_u(k)
 
-        weave(3, 2, 4, True)
+        mul_grad(0, range(3, 4))
+        mul_grad(1, range(3, 4))
         quant_x(3, 2, 4)
-        for j in range(2):
-            mul_grad(j, range(GROUPS))
         for k in range(1, GROUPS):
-            for t in range(2, 4):
-                widen(k, t, 1)
-            weave(k, 4, 6, k in ())
-        weaves = {1: [(1, 6, 8)], 2: [(2, 6, 8)], 3: [(3, 6, 8)]}
+            for t in range(WIDE[k], 4):
+                widen(k, t, 1, 2)
+            weave(k, 4, 6, False)
         quants = {0: [(1, 4, 6)], 1: [(2, 4, 6), (3, 4, 6)], 2: [(1, 6, 8)], 3: [(2, 6, 8)], 4: [(3, 6, 8)]}
         for j in range(DT + 3):
             if j < DT:
@@ -341,17 +324,17 @@ def tile_adalorasensitivityscore_w4_kernel(tc, x_bytes, x_scale, g, p, lam, q_wo
                 abs_s(j)
                 place_a(j)
             if 2 <= j < DT + 2:
-                new_u(j - 2)
-            if j < DT and j not in TENSOR_W and j not in GPSIMD_W:
+                add_u(j - 2)
+            if j < DT and j not in TENSOR_W:
                 place_u(j)
             if 1 <= j <= DT:
-                new_i(j - 1)
-                diff(j - 1)
+                add_a(j - 1)
+                minus_a(j - 1)
                 abs_e(j - 1)
             if j >= 3:
                 finish(j - 3)
-            for unit in weaves.get(j, []):
-                weave(*unit, False)
+            if 1 <= j < GROUPS:
+                weave(j, 6, 8, False)
             for unit in quants.get(j, []):
                 quant_x(*unit)
             if j + 2 < DT:

from contextlib import ExitStack

import concourse.mybir as mybir
from concourse.masks import make_identity

T, D, F, R = 2048, 1024, 1024, 512
FLOPS = 2 * T * F * R + 2 * T * D * R
BYTES = T * D + 4 * T + 2 * T * F + 3 * 2 * D * R + 2 * R + F * R // 2 + F * R // 32 + 4 * D * R

F32 = mybir.dt.float32
BF16 = mybir.dt.bfloat16
I32 = mybir.dt.int32
U32 = mybir.dt.uint32
U8 = mybir.dt.uint8
FP8 = mybir.dt.float8_e4m3fn
FP8X4 = mybir.dt.float8_e4m3fn_x4
FP4X4 = mybir.dt.float4_e2m1fn_x4
ACT = mybir.ActivationFunctionType
ALU = mybir.AluOpType

P = 128
PACK = 4
GROUPS = T // 512
FP = F // 512
DT = D // P
HALF = D // 2
TENSOR_W = (0, 2, 3, 5, 6)
WIDE = (0, 2, 2, 2)
SQRT_T_INV = float(T) ** -0.5


def tile_adalorasensitivityscore_w4_kernel(tc, x_bytes, x_scale, g, p, lam, q_words, q_scales, avg_i, avg_u, out):
    nc = tc.nc
    with ExitStack() as ctx:
        keep = ctx.enter_context(tc.tile_pool(name="keep", bufs=1))
        pair = ctx.enter_context(tc.tile_pool(name="pair", bufs=2))
        quad = ctx.enter_context(tc.tile_pool(name="quad", bufs=4))
        work = ctx.enter_context(tc.tile_pool(name="work", bufs=3))
        ps_t = ctx.enter_context(tc.psum_pool(name="ps_t", bufs=4))
        ps_u = ctx.enter_context(tc.psum_pool(name="ps_u", bufs=4))
        ctx.enter_context(tc.manual_schedule())

        warm = keep.tile([P, 1], F32, name="warm")
        lam_row = keep.tile([P, R], BF16, name="lam_row")
        ones = keep.tile([P, P], BF16, name="ones")
        ident = keep.tile([P, P], F32, name="ident")
        ident_b = keep.tile([P, P], BF16, name="ident_b")
        lam_all = keep.tile([P, R], F32, name="lam_all")
        x_s = keep.tile([P, GROUPS, PACK], F32, name="x_s")
        q_w = keep.tile([P, FP, 2 * R], U8, align_bytes=64, name="q_w")
        q_s = keep.tile([P, FP * R], U8, align_bytes=64, name="q_s")

        nc.vector.memset(warm[:], 0.0)
        nc.vector.memset(q_s[:].bitcast(I32), 0)
        nc.gpsimd.memset(lam_row[:], 0.0)
        nc.gpsimd.memset(ones[:], 1.0)
        make_identity(nc, ident[:])
        nc.gpsimd.tensor_copy(out=ident_b[:], in_=ident[:])
        nc.scalar.dma_start(out=x_s[:], in_=x_scale.rearrange("(g p t) o -> p g (t o)", p=P, t=PACK))
        nc.scalar.dma_start(out=lam_row[0:1, :], in_=lam.rearrange("(o r) -> o r", o=1))
        nc.scalar.activation(out=warm[:], in_=warm[:], func=ACT.Abs)

        x_view = x_bytes.rearrange("(g p t) n -> g p t n", p=P, t=PACK)
        g_view = g.rearrange("(g p t) f -> g p t f", p=P, t=PACK)
        x_b = [keep.tile([P, PACK, D], U8, name=f"x_b{k}") for k in range(GROUPS)]
        g_sb = [[keep.tile([P, F], BF16, name=f"g_sb{k}_{t}") for t in range(PACK)] for k in range(GROUPS)]
        for t0, t1 in ((0, 1), (1, 2), (2, 4)):
            nc.sync.dma_start(out=x_b[0][:, t0:t1, :], in_=x_view[0][:, t0:t1, :])
        for k in range(GROUPS):
            for t in range(PACK):
                nc.sync.dma_start(out=g_sb[k][t][:], in_=g_view[k][:, t, :])
            if k > 0:
                nc.sync.dma_start(out=x_b[k][:], in_=x_view[k])
            else:
                nc.sync.dma_start(out=q_w[:], in_=q_words.rearrange("g p n -> p g n"))
                for b in range(4):
                    nc.sync.dma_start(
                        out=q_s[32 * b : 32 * b + 4, :].bitcast(I32).rearrange("p (g n) -> p g n", g=FP),
                        in_=q_scales.bitcast(I32).rearrange("g (b r) n -> b r g n", r=4)[b],
                    )
        epi = {}
        for h in range(2):
            for name, src in (("p", p), ("a", avg_i), ("u", avg_u)):
                epi[name, h] = keep.tile([P, DT // 2, R], BF16, name=f"{name}_sb{h}")
                nc.sync.dma_start(out=epi[name, h][:], in_=src.rearrange("(h j p) r -> h p j r", p=P, h=2)[h])

        def rows_of(name, j):
            return epi[name, j // 4][:, j % 4, :]

        turned = {}
        g_x = {}
        g_c = {}
        g_s = {}

        def turn_g(k, t):
            bank = ps_t.tile([P, FP, 2, P], F32, name="bank_t")
            words = g_sb[k][t][:].bitcast(F32)
            for f in range(FP):
                for u in range(2):
                    nc.tensor.transpose(bank[:, f, u, :], words[:, 256 * f + u : 256 * (f + 1) : 2], ident[:])
            turned[k, t] = bank

        def unload_g(k, t):
            if t == 0:
                g_x[k] = pair.tile([P, PACK, FP, P, PACK], BF16, align_bytes=64, name="g_x")
            dst = g_x[k][:, t].rearrange("p f r t -> p f (r t)").bitcast(F32)
            nc.scalar.copy(
                out=dst.rearrange("p f (r u) -> p f r u", u=2),
                in_=turned[k, t][:].rearrange("p f u r -> p f r u"),
            )

        def quant_g(k):
            g_c[k] = pair.tile([P, PACK, FP, P], U32, align_bytes=64, name="g_c")
            g_s[k] = pair.tile([P, PACK, FP, P], U8, align_bytes=64, name="g_s")
            nc.vector.quantize_mx(
                out=g_c[k][:].rearrange("p a f r -> p (a f r)").bitcast(FP8X4),
                scales=g_s[k][:].rearrange("p a f r -> p (a f r)"),
                in_=g_x[k][:].rearrange("p a f r t -> p (a f r t)"),
            )

        u_bank = {}
        ul_x = {}
        ul_c = [keep.tile([P, R], U32, align_bytes=64, name=f"ul_c{k}") for k in range(GROUPS)]
        ul_s = [keep.tile([P, R], U8, align_bytes=64, name=f"ul_s{k}") for k in range(GROUPS)]

        def mul_u(k, c):
            bank = ps_u.tile([P, PACK, P], F32, name="bank_u")
            for t in range(PACK):
                for f in range(FP):
                    nc.tensor.matmul_mx(
                        out=bank[:, t, :],
                        lhsT=g_c[k][:, t, f, :].bitcast(FP8X4),
                        lhsT_scale=g_s[k][:, t, f, :],
                        rhs=q_w[:, f, 2 * P * c : 2 * P * (c + 1)].bitcast(FP4X4),
                        rhs_scale=q_s[:, R * f + P * c : R * f + P * (c + 1)],
                        start=(f == 0),
                        stop=(f == FP - 1),
                    )
            u_bank[k, c] = bank

        def scale_u(k, c):
            if c == 0:
                ul_x[k] = pair.tile([P, R, PACK], BF16, align_bytes=64, name="ul_x")
            cols = slice(P * c, P * (c + 1))
            nc.vector.tensor_tensor(
                out=ul_x[k][:, cols, :],
                in0=u_bank[k, c][:].rearrange("p t r -> p r t"),
                in1=lam_all[:, cols].unsqueeze(2).to_broadcast([P, P, PACK]),
                op=ALU.mult,
            )

        def quant_u(k):
            nc.vector.quantize_mx(
                out=ul_c[k][:].bitcast(FP8X4),
                scales=ul_s[k][:],
                in_=ul_x[k][:].rearrange("p r t -> p (r t)"),
            )

        x_w = [keep.tile([P, PACK, D], BF16, align_bytes=64, name=f"x_w{k}") for k in range(GROUPS)]
        x_x = {}
        x_c = {}
        x_q = {}

        def widen(k, t, h0, h1, on_vector=False):
            cols = slice(HALF * h0, HALF * h1)
            src = x_b[k][:, t, cols].bitcast(FP8)
            dst = x_w[k][:, t, cols]
            col = x_s[:, k, t : t + 1]
            if on_vector:
                nc.vector.tensor_scalar(out=dst, in0=src, scalar1=col, scalar2=None, op0=ALU.mult)
            else:
                nc.scalar.activation(out=dst, in_=src, func=ACT.Copy, scale=col)

        def weave(k, j0, j1, on_vector):
            n = P * (j1 - j0)
            if (k, j0) not in x_x:
                x_x[k, j0] = (quad, pair)[n == HALF].tile([P, n, PACK], BF16, align_bytes=64, name=f"x_x{j1 - j0}")
            src = x_w[k][:, :, P * j0 : P * j1].rearrange("p t (n i) -> p n t i", i=4)
            dst = x_x[k, j0][:].rearrange("p (n i) t -> p n t i", i=4)
            if on_vector:
                nc.vector.tensor_copy(out=dst, in_=src)
            else:
                nc.scalar.copy(out=dst, in_=src)

        def quant_x(k, j0, j1):
            n = P * (j1 - j0)
            codes = keep.tile([P, n], U32, align_bytes=64, name=f"x_c{k}_{j0}")
            scales = keep.tile([P, n], U8, align_bytes=64, name=f"x_q{k}_{j0}")
            nc.vector.quantize_mx(
                out=codes[:].bitcast(FP8X4),
                scales=scales[:],
                in_=x_x[k, j0][:].rearrange("p n t -> p (n t)"),
            )
            for j in range(j0, j1):
                cols = slice(P * (j - j0), P * (j - j0 + 1))
                x_c[k, j] = codes[:, cols]
                x_q[k, j] = scales[:, cols]

        grad = {}
        a_bank = {}
        u_new = {}
        y, s, d, e, i_new = {}, {}, {}, {}, {}

        def mul_grad(j, groups):
            if groups[0] == 0:
                grad[j] = ps_u.tile([P, R], F32, name="bank_u")
            for k in groups:
                nc.tensor.matmul_mx(
                    out=grad[j][:],
                    lhsT=x_c[k, j].bitcast(FP8X4),
                    lhsT_scale=x_q[k, j],
                    rhs=ul_c[k][:].bitcast(FP8X4),
                    rhs_scale=ul_s[k][:],
                    start=(k == 0),
                    stop=(k == GROUPS - 1),
                )

        def times_p(j):
            y[j] = work.tile([P, R], F32, name="y")
            nc.vector.tensor_tensor(out=y[j][:], in0=grad[j][:], in1=rows_of("p", j), op=ALU.mult)

        def abs_s(j):
            s[j] = work.tile([P, R], F32, name="s")
            nc.scalar.activation(out=s[j][:], in_=y[j][:], func=ACT.Abs, scale=3.0 / 7.0 * SQRT_T_INV)

        def place_a(j):
            a_bank[j] = ps_t.tile([P, R], F32, name="bank_t")
            nc.tensor.matmul(a_bank[j][:], ident_b[:], rows_of("a", j), start=True, stop=True)

        def add_a(j):
            i_new[j] = work.tile([P, R], F32, name="i_new")
            nc.gpsimd.tensor_tensor(out=i_new[j][:], in0=s[j][:], in1=rows_of("a", j), op=ALU.add)

        def minus_a(j):
            d[j] = work.tile([P, R], F32, name="d")
            nc.vector.scalar_tensor_tensor(out=d[j][:], in0=s[j][:], scalar=7.0 / 3.0, in1=a_bank[j][:], op0=ALU.mult, op1=ALU.subtract)

        def abs_e(j):
            e[j] = work.tile([P, R], F32, name="e")
            nc.scalar.activation(out=e[j][:], in_=d[j][:], func=ACT.Abs, scale=0.3)

        def place_u(j):
            u_new[j] = ps_u.tile([P, R], F32, name="bank_u")
            nc.tensor.matmul(u_new[j][:], ident_b[:], rows_of("u", j), start=True, stop=True)

        def add_u(j):
            if j in TENSOR_W:
                w = ps_t.tile([P, R], F32, name="bank_t")
                nc.tensor.matmul(w[:], ident_b[:], rows_of("u", j), start=True, stop=False)
                nc.tensor.matmul(w[:], ident[:], e[j][:], start=False, stop=True)
            else:
                w = pair.tile([P, R], F32, name="w")
                nc.vector.tensor_tensor(out=w[:], in0=u_new[j][:], in1=e[j][:], op=ALU.add)
            u_new[j] = w

        def finish(j):
            o = work.tile([P, R], F32, name="o")
            parts = 2 if j == DT - 1 else 1
            for i in range(parts):
                cols = slice(R // parts * i, R // parts * (i + 1))
                nc.vector.scalar_tensor_tensor(
                    out=o[:, cols], in0=u_new[j][:, cols], scalar=0.49, in1=i_new[j][:, cols], op0=ALU.mult, op1=ALU.mult
                )
                nc.sync.dma_start(out=out[P * j : P * (j + 1), cols], in_=o[:, cols])

        lam_bank = ps_u.tile([P, R], F32, name="bank_u")
        nc.tensor.matmul(lam_bank[:], ones[:], lam_row[:], start=True, stop=True)
        for t in range(PACK):
            widen(0, t, 0, 1, on_vector=True)
        for t in range(3):
            widen(0, t, 1, 2)
        for t in range(PACK):
            turn_g(0, t)
            unload_g(0, t)
        nc.scalar.copy(out=lam_all[:], in_=lam_bank[:])
        weave(0, 0, 4, True)
        widen(0, 3, 1, 2, on_vector=True)
        quant_x(0, 0, 4)
        weave(0, 4, 8, True)
        quant_g(0)
        quant_x(0, 4, 8)

        for k in range(GROUPS):
            n = k + 1
            if n < GROUPS:
                for t in range(PACK):
                    turn_g(n, t)
                    unload_g(n, t)
                    if n > 1 and t in (1,):
                        widen(n, t, 0, 2 if t < WIDE[n] else 1)
                for t in range(PACK):
                    if n == 1 or t not in (1,):
                        widen(n, t, 0, 2 if t < WIDE[n] else 1)
            for c in range(4):
                mul_u(k, c)
            if k > 0:
                weave(k, 0, 4 if k < 3 else 2, True)
            scale_u(k, 0)
            scale_u(k, 1)
            if k > 0:
                quant_x(k, 0, 4 if k < 3 else 2)
            if k == 3:
                mul_grad(0, range(3))
                mul_grad(1, range(3))
            scale_u(k, 2)
            scale_u(k, 3)
            if n < GROUPS:
                quant_g(n)
            else:
                weave(3, 2, 4, True)
            quant_u(k)

        mul_grad(0, range(3, 4))
        mul_grad(1, range(3, 4))
        quant_x(3, 2, 4)
        for k in range(1, GROUPS):
            for t in range(WIDE[k], 4):
                widen(k, t, 1, 2)
            weave(k, 4, 6, False)
        quants = {0: [(1, 4, 6)], 1: [(2, 4, 6), (3, 4, 6)], 2: [(1, 6, 8)], 3: [(2, 6, 8)], 4: [(3, 6, 8)]}
        for j in range(DT + 3):
            if j < DT:
                times_p(j)
                abs_s(j)
                place_a(j)
            if 2 <= j < DT + 2:
                add_u(j - 2)
            if j < DT and j not in TENSOR_W:
                place_u(j)
            if 1 <= j <= DT:
                add_a(j - 1)
                minus_a(j - 1)
                abs_e(j - 1)
            if j >= 3:
                finish(j - 3)
            if 1 <= j < GROUPS:
                weave(j, 6, 8, False)
            for unit in quants.get(j, []):
                quant_x(*unit)
            if j + 2 < DT:
                mul_grad(j + 2, range(GROUPS))
